import numpy as np
import ml_dtypes


def mxq(x, axis, fmt="e4m3"):
    dtype, down = {"e4m3": (ml_dtypes.float8_e4m3fn, 7), "e5m2": (ml_dtypes.float8_e5m2, 14)}[fmt]
    v = np.moveaxis(np.asarray(x, np.float32).astype(ml_dtypes.bfloat16).astype(np.float64), axis, -1)
    blocks = v.reshape(v.shape[:-1] + (-1, 32))
    amax = np.abs(blocks).max(-1, keepdims=True)
    byte = np.maximum(np.where(amax > 0, np.frexp(amax)[1] - 1 + 127, 0) - down, 1)
    scale = np.exp2(byte - 127.0)
    codes = (blocks / scale).astype(np.float32).astype(dtype).astype(np.float64)
    return np.moveaxis((codes * scale).reshape(v.shape), -1, axis)


WIDE = False


def mx_kscale(k):
    if not WIDE:
        return np.ones(k)
    levels = np.array([30, -30])
    if k % 512:
        return np.exp2(np.random.permutation(np.resize(levels, k // 32))).repeat(32)
    a = np.empty((k // 512, 16))
    for p in range(k // 512):
        a[p, :8] = np.random.permutation(np.resize(levels, 8))
        for g in range(8):
            far = levels[np.abs(levels - a[p, g]) >= 10]
            a[p, g + 8] = far[np.random.randint(len(far))]
    return np.exp2(a.ravel()).repeat(32)


def f64(x):
    return np.asarray(x).astype(np.float64)


def striped(idx):
    return np.tile(np.asarray(idx).reshape(-1, 16).T, (8, 1)).astype(np.uint16)


def unstriped(offs):
    return offs[:16].T.reshape(-1).astype(np.int64)


E2M1 = np.array([0.0, 0.5, 1.0, 1.5, 2.0, 3.0, 4.0, 6.0, -0.0, -0.5, -1.0, -1.5, -2.0, -3.0, -4.0, -6.0])


def pack_weight(w, fmt):
    k, n = w.shape
    w = f64(np.asarray(w, np.float32).astype(ml_dtypes.bfloat16)).reshape(k // 32, 32, n)
    amax = np.abs(w).max(1)
    if fmt == "e4m3":
        byte = np.frexp(amax)[1] - 1 + 127 - 7
    else:
        mant, ex = np.frexp(amax / 6.0)
        byte = np.where(mant > 0.5, ex, ex - 1) + 127
    byte = np.clip(np.where(amax > 0, byte, 1), 1, 254)
    scaled = (w * np.exp2(127.0 - byte)[:, None, :]).reshape(k, n).astype(np.float32)
    by_word = np.ascontiguousarray(scaled.reshape(k // 512, 128, 4, n).transpose(0, 1, 3, 2))
    if fmt == "e4m3":
        words = by_word.astype(ml_dtypes.float8_e4m3fn).view(np.uint8)
    else:
        c = by_word.astype(ml_dtypes.float4_e2m1fn).view(np.uint8) & 0xF
        words = (c[..., 0::2] | (c[..., 1::2] << 4)).reshape(k // 512, 128, 2 * n)
    return np.ascontiguousarray(words), np.ascontiguousarray(byte.astype(np.uint8).reshape(k // 512, 16, n))


def unpack_weight(words, scales, fmt):
    g, _, n = scales.shape
    words = np.ascontiguousarray(words).reshape(g, 128, n, -1)
    if fmt == "e4m3":
        vals = words.view(ml_dtypes.float8_e4m3fn).astype(np.float64)
    else:
        nib = np.empty((g, 128, n, 4), np.uint8)
        nib[..., 0::2] = words & 0xF
        nib[..., 1::2] = words >> 4
        vals = E2M1[nib]
    vals = vals * np.repeat(np.exp2(scales.astype(np.float64) - 127.0), 8, axis=1)[..., None]
    return vals.transpose(0, 1, 3, 2).reshape(g * 512, n)


def bf(x):
    return np.asarray(x, np.float32).astype(ml_dtypes.bfloat16)


def planes(Y):
    r, m = Y.shape
    b = f64(bf(Y)).reshape(r // 32, 32, m)
    amax = np.abs(b).max(1)
    byte = np.clip(np.where(amax > 0, np.frexp(amax)[1] - 1 + 127 - 7, 1), 1, 254)
    codes = (b * np.exp2(127.0 - byte)[:, None, :]).reshape(r, m).astype(np.float32).astype(ml_dtypes.float8_e4m3fn).view(np.uint8)
    words = codes.reshape(r // 512, 128, 4, m).transpose(0, 1, 3, 2)
    return np.ascontiguousarray(words), np.ascontiguousarray(byte.astype(np.uint8).reshape(r // 512, 16, m))


K, T, J, R, C, O, N = 1024, 1024, 256, 512, 1024, 256, 512


def setup_inputs():
    n = np.random.standard_normal
    idx = np.random.permutation(T)[:J]
    idx2 = np.random.permutation(C)[:J]
    idx3 = np.random.permutation(C)[:O]
    fk = mx_kscale(K)
    fr = mx_kscale(R)
    wp = pack_weight(n((K, R)) * 1 / np.sqrt(K) * fk[:, None] * fr, "e4m3")
    wbp = pack_weight(n((R, N)) * 1 / np.sqrt(R) / fr[:, None], "e2m1")
    return {
        "xf": (n((K, T))).astype(np.float32),
        "fk": (np.random.uniform(0.5, 2.0, (K, 1)) / fk[:, None]).astype(np.float32),
        "w_words": wp[0],
        "w_scales": wp[1],
        "oldh": (n((R, C)) * 0.7 * fr[:, None]).astype(np.float32),
        "wb_words": wbp[0],
        "wb_scales": wbp[1],
        "rs": (n((N, O))).astype(np.float32),
        "offs": striped(idx),
        "offs2": striped(idx2),
        "offs3": striped(idx3),
    }


def reference(xf, fk, w_words, w_scales, oldh, wb_words, wb_scales, rs, offs, offs2, offs3):
    idx = unstriped(offs)
    idx2 = unstriped(offs2)
    idx3 = unstriped(offs3)
    wu = unpack_weight(w_words, w_scales, "e4m3")
    wbu = unpack_weight(wb_words, wb_scales, "e2m1")
    xg = f64(xf)[:, idx]
    x1 = np.pad(xg, ((0, 0), (1, 0)))[:, :J]
    u = (xg - 0.6 * x1) * f64(fk)
    uq = mxq(u, 0, "e4m3")
    a = wu.T @ uq
    ha = np.maximum(a, 0.0)
    pw0 = np.zeros((R, C))
    pw0[:, idx2] = ha
    pg = pw0 + f64(oldh)
    hid = pg[:, idx3]
    hidq = mxq(hid, 0, "e5m2")
    p = wbu.T @ hidq
    p1 = np.pad(p, ((0, 0), (1, 0)))[:, :O]
    y = p - 0.7 * p1 + 0.5 * f64(rs)
    words, scales = planes(y)
    return y, words, scales

@@ -1,0 +1,227 @@
+from contextlib import ExitStack
+
+import concourse.mybir as mybir
+
+K, T, J, R, C, O, N = 1024, 1024, 256, 512, 1024, 256, 512
+FLOPS = 2 * K * R * J + 2 * R * N * O
+
+F32 = mybir.dt.float32
+BF16 = mybir.dt.bfloat16
+I32 = mybir.dt.int32
+U32 = mybir.dt.uint32
+U16 = mybir.dt.uint16
+U8 = mybir.dt.uint8
+E4M3X4 = mybir.dt.float8_e4m3fn_x4
+E5M2X4 = mybir.dt.float8_e5m2_x4
+E2M1X4 = mybir.dt.float4_e2m1fn_x4
+MULT = mybir.AluOpType.mult
+ADD = mybir.AluOpType.add
+MAX = mybir.AluOpType.max
+COPY = mybir.ActivationFunctionType.Copy
+RELU = mybir.ActivationFunctionType.Relu
+
+P = 128
+PACK = 4
+K_PASS = P * PACK
+PASSES = K // K_PASS
+LEAD = 4
+HALF = O // 2
+U_SPLIT = 176
+
+
+def tile_list_page_steps_lagged_pl_kernel(
+    tc, xf, fk, w_words, w_scales, oldh, wb_words, wb_scales, rs, offs, offs2, offs3, out_0, out_1, out_2
+):
+    nc = tc.nc
+    with ExitStack() as ctx:
+        lists = ctx.enter_context(tc.tile_pool(name="lists", bufs=1))
+        pool = ctx.enter_context(tc.tile_pool(name="pool", bufs=1))
+        psum = ctx.enter_context(tc.psum_pool(name="psum", bufs=1))
+
+        def sb(shape, dtype, name):
+            return pool.tile(shape, dtype, name=name, align_bytes=64)
+
+        token_list = lists.tile([P, J // 16], U16, name="token_list")
+        place_list = lists.tile([P, J // 16], U16, name="place_list")
+        read_list = lists.tile([P, O // 16], U16, name="read_list")
+
+        nc.sync.dma_start(token_list[:], offs)
+        factor = sb([P, PASSES, PACK], F32, "factor")
+        nc.scalar.dma_start(factor[:], fk.rearrange("(a p t) o -> p a (t o)", a=PASSES, t=PACK))
+        x_rows = {}
+        wb_raw = sb([P, 2 * N], U8, "wb_raw")
+        for a in range(PASSES):
+            for t in range(PACK):
+                x_rows[a, t] = sb([P, T], F32, "x_rows_%d_%d" % (a, t))
+                nc.sync.dma_start(x_rows[a, t][:], xf[a * K_PASS + t : (a + 1) * K_PASS : PACK, :])
+            if a == 0:
+                nc.sync.dma_start(wb_raw[:].bitcast(I32), wb_words[0].bitcast(I32))
+        w_raw = []
+        for a in range(PASSES):
+            w_raw.append(sb([P, R], I32, "w_raw_%d" % a))
+            nc.sync.dma_start(w_raw[a][:], w_words[a].rearrange("p c r -> p (c r)").bitcast(I32))
+        nc.sync.dma_start(place_list[:], offs2)
+        nc.sync.dma_start(read_list[:], offs3)
+        old = []
+        for t in range(PACK):
+            old.append(sb([P, C], F32, "old_%d" % t))
+            nc.sync.dma_start(old[t][:], oldh[t:R:PACK, :])
+        lag = sb([P, PACK, O], F32, "lag")
+        nc.sync.dma_start(lag[:], rs.rearrange("(p t) o -> p t o", t=PACK))
+
+        scale_raw = sb([P, PASSES + 1, R], U8, "scale_raw")
+        nc.gpsimd.memset(scale_raw[:].rearrange("p m c -> p (m c)").bitcast(I32), 0)
+        for q in range(4):
+            nc.gpsimd.dma_start(
+                scale_raw[32 * q : 32 * q + 4, 0:PASSES, :].bitcast(I32),
+                w_scales[:, 4 * q : 4 * q + 4, :].rearrange("a r c -> r a c").bitcast(I32),
+            )
+        for q in range(4):
+            nc.gpsimd.dma_start(
+                scale_raw[32 * q : 32 * q + 4, PASSES, :].bitcast(I32),
+                wb_scales[0, 4 * q : 4 * q + 4, :].bitcast(I32),
+            )
+
+        scaled = []
+        for a in range(PASSES):
+            scaled.append(sb([P, PACK, LEAD + J], F32, "scaled_%d" % a))
+            nc.vector.memset(scaled[a][:, :, LEAD - 1 : LEAD], 0.0)
+        placed = []
+        for t in range(PACK):
+            placed.append(sb([P, C], F32, "placed_%d" % t))
+            nc.vector.memset(placed[t][:], 0.0)
+
+        u_codes, u_scales = [], []
+        scale_dealt = sb([P, PASSES + 1, PACK, P], U8, "scale_dealt")
+        wb_dealt = sb([P, PACK, 2 * P], U8, "wb_dealt")
+        w_dealt = [sb([P, PACK, P], I32, "w_dealt_%d" % a) for a in range(PASSES)]
+
+        def deal_w(a):
+            nc.vector.tensor_copy(
+                w_dealt[a][:].rearrange("p t q -> p q t"), w_raw[a][:].rearrange("p (q t) -> p q t", t=PACK)
+            )
+
+        for a in range(PASSES):
+            u_rows = sb([P, PACK, J], BF16, "u_rows_%d" % a)
+            for t in range(PACK):
+                picked = sb([P, J], F32, "picked_%d_%d" % (a, t))
+                nc.scalar.activation(picked[:], x_rows[a, t][:].indirect(token_list[:]), COPY)
+                nc.scalar.activation(scaled[a][:, t, LEAD:], picked[:], COPY, scale=factor[:, a, t : t + 1])
+                if a == PASSES - 1 and t == PACK - 1:
+                    deal_w(0)
+                nc.vector.scalar_tensor_tensor(
+                    u_rows[:, t, :], scaled[a][:, t, LEAD - 1 : LEAD - 1 + J], -0.6, scaled[a][:, t, LEAD:], MULT, ADD
+                )
+            if a == PASSES - 1:
+                deal_w(1)
+            u_words = sb([P, J, PACK], BF16, "u_words_%d" % a)
+            nc.vector.tensor_copy(u_words[:, :U_SPLIT, :], u_rows[:, :, :U_SPLIT].rearrange("p t j -> p j t"))
+            nc.scalar.copy(u_words[:, U_SPLIT:, :], u_rows[:, :, U_SPLIT:].rearrange("p t j -> p j t"))
+            u_codes.append(sb([P, J], U32, "u_codes_%d" % a))
+            u_scales.append(sb([P, J], U8, "u_scales_%d" % a))
+            nc.vector.quantize_mx(
+                out=u_codes[a][:].bitcast(E4M3X4), scales=u_scales[a][:], in_=u_words[:].rearrange("p j t -> p (j t)")
+            )
+            if a == 0:
+                nc.vector.tensor_copy(
+                    scale_dealt[:].rearrange("p m t q -> p m q t"),
+                    scale_raw[:].rearrange("p m (q t) -> p m q t", t=PACK),
+                )
+                nc.vector.tensor_copy(
+                    wb_dealt[:].rearrange("p t (q b) -> p q t b", b=2),
+                    wb_raw[:].rearrange("p (q t b) -> p q t b", t=PACK, b=2),
+                )
+
+        first = [psum.tile([P, J], F32, name="first_%d" % t) for t in range(PACK)]
+        for a in range(PASSES):
+            for t in range(PACK):
+                nc.tensor.matmul_mx(
+                    out=first[t][:],
+                    lhsT=w_dealt[a][:, t, :].bitcast(E4M3X4),
+                    lhsT_scale=scale_dealt[:, a, t, :],
+                    rhs=u_codes[a][:].bitcast(E4M3X4),
+                    rhs_scale=u_scales[a][:],
+                    start=(a == 0),
+                    stop=(a == PASSES - 1),
+                )
+
+        ha = [sb([P, J], F32, "ha_%d" % t) for t in range(PACK)]
+        page = [sb([P, C], F32, "page_%d" % t) for t in range(PACK)]
+        hid_rows = sb([P, PACK, O], BF16, "hid_rows")
+
+        def relu_on_vector(t):
+            nc.vector.tensor_scalar(ha[t][:], first[t][:], 0.0, None, MAX)
+
+        def place_on_scalar(t):
+            nc.scalar.activation(placed[t][:].indirect(place_list[:]), ha[t][:], COPY)
+
+        nc.scalar.activation(ha[0][:], first[0][:], RELU)
+        place_on_scalar(0)
+        relu_on_vector(1)
+        relu_on_vector(2)
+        nc.vector.tensor_copy(placed[1][:].indirect(place_list[:]), ha[1][:])
+        relu_on_vector(3)
+        place_on_scalar(2)
+        place_on_scalar(3)
+        for t in range(PACK):
+            nc.vector.tensor_tensor(page[t][:], placed[t][:], old[t][:], ADD)
+        for t in range(PACK - 1):
+            nc.scalar.activation(hid_rows[:, t, :], page[t][:].indirect(read_list[:]), COPY)
+        last = PACK - 1
+        nc.vector.tensor_copy(hid_rows[:, last, :HALF], page[last][:].indirect(read_list[:, : HALF // 16]))
+        nc.scalar.activation(hid_rows[:, last, HALF:], page[last][:].indirect(read_list[:, HALF // 16 :]), COPY)
+
+        second = [psum.tile([P, PACK, HALF], F32, name="second_%d" % h) for h in range(2)]
+        for h in range(2):
+            cols = slice(h * HALF, (h + 1) * HALF)
+            hid_words = sb([P, HALF, PACK], BF16, "hid_words_%d" % h)
+            if h == 0:
+                nc.vector.tensor_copy(hid_words[:], hid_rows[:, :, cols].rearrange("p t o -> p o t"))
+            else:
+                nc.scalar.copy(hid_words[:], hid_rows[:, :, cols].rearrange("p t o -> p o t"))
+            hid_codes = sb([P, HALF], U32, "hid_codes_%d" % h)
+            hid_scales = sb([P, HALF], U8, "hid_scales_%d" % h)
+            nc.vector.quantize_mx(
+                out=hid_codes[:].bitcast(E5M2X4), scales=hid_scales[:], in_=hid_words[:].rearrange("p o t -> p (o t)")
+            )
+            for t in range(PACK):
+                nc.tensor.matmul_mx(
+                    out=second[h][:, t, :],
+                    lhsT=wb_dealt[:, t, :].bitcast(E2M1X4),
+                    lhsT_scale=scale_dealt[:, PASSES, t, :],
+                    rhs=hid_codes[:].bitcast(E5M2X4),
+                    rhs_scale=hid_scales[:],
+                    start=True,
+                    stop=True,
+                )
+
+        y_codes = sb([P, O], U32, "y_codes")
+        y_scales = sb([P, O], U8, "y_scales")
+        out_rows = out_0.rearrange("(p t) o -> p t o", t=PACK)
+        y_words = []
+        for h in range(2):
+            cols = slice(h * HALF, (h + 1) * HALF)
+            width = min(HALF, O - 1 - h * HALF)
+            ahead = lag[:, :, h * HALF + 1 : h * HALF + 1 + width]
+            nc.vector.scalar_tensor_tensor(ahead, second[h][:, :, :width], -1.4, ahead, MULT, ADD)
+            y = sb([P, PACK, HALF], F32, "y_%d" % h)
+            nc.vector.scalar_tensor_tensor(y[:], lag[:, :, cols], 0.5, second[h][:], MULT, ADD)
+            nc.sync.dma_start(out_rows[:, :, cols], y[:])
+            y_words.append(sb([P, HALF, PACK], BF16, "y_words_%d" % h))
+            if h == 0:
+                nc.scalar.copy(y_words[h][:], y[:].rearrange("p t o -> p o t"))
+            else:
+                nc.vector.tensor_copy(y_words[h][:], y[:].rearrange("p t o -> p o t"))
+        for h in range(2):
+            cols = slice(h * HALF, (h + 1) * HALF)
+            nc.vector.quantize_mx(
+                out=y_codes[:, cols].bitcast(E4M3X4),
+                scales=y_scales[:, cols],
+                in_=y_words[h][:].rearrange("p o t -> p (o t)"),
+            )
+        nc.sync.dma_start(out_1[0].rearrange("p c r -> p (c r)").bitcast(I32), y_codes[:].bitcast(I32))
+        for q in range(4):
+            engine = nc.scalar if q % 2 == 0 else nc.sync
+            engine.dma_start(
+                out_2[0, 4 * q : 4 * q + 4, :].bitcast(I32), y_scales[32 * q : 32 * q + 4, :].bitcast(I32)
+            )

@@ -26,7 +26,9 @@ K_PASS = P * PACK
 PASSES = K // K_PASS
 LEAD = 4
 HALF = O // 2
-U_SPLIT = 176
+U_SPLIT = 192
+PICK_SPLIT = 160
+Y_SPLIT = 80
 
 
 def tile_list_page_steps_lagged_pl_kernel(
@@ -47,15 +49,34 @@ def tile_list_page_steps_lagged_pl_kernel(
 
         nc.sync.dma_start(token_list[:], offs)
         factor = sb([P, PASSES, PACK], F32, "factor")
-        nc.scalar.dma_start(factor[:], fk.rearrange("(a p t) o -> p a (t o)", a=PASSES, t=PACK))
-        x_rows = {}
+        scale_raw = sb([P, R], U8, "scale_raw")
         wb_raw = sb([P, 2 * N], U8, "wb_raw")
-        for a in range(PASSES):
-            for t in range(PACK):
-                x_rows[a, t] = sb([P, T], F32, "x_rows_%d_%d" % (a, t))
-                nc.sync.dma_start(x_rows[a, t][:], xf[a * K_PASS + t : (a + 1) * K_PASS : PACK, :])
-            if a == 0:
-                nc.sync.dma_start(wb_raw[:].bitcast(I32), wb_words[0].bitcast(I32))
+        x_rows = {}
+
+        def load_x(a, t0, t1):
+            chunk = sb([P, t1 - t0, T], F32, "x_rows_%d_%d" % (a, t0))
+            nc.sync.dma_start(
+                chunk[:], xf[a * K_PASS : (a + 1) * K_PASS, :].rearrange("(p t) c -> p t c", t=PACK)[:, t0:t1, :]
+            )
+            for t in range(t0, t1):
+                x_rows[a, t] = chunk[:, t - t0, :]
+
+        load_x(0, 0, 1)
+        nc.sync.dma_start(factor[:], fk.rearrange("(a p t) o -> p a (t o)", a=PASSES, t=PACK))
+        load_x(0, 1, 2)
+        load_x(0, 2, 4)
+        for q in range(4):
+            nc.sync.dma_start(
+                scale_raw[32 * q + 4 : 32 * q + 12, :].bitcast(I32), w_scales[:, 4 * q : 4 * q + 4, :].bitcast(I32)
+            )
+        load_x(1, 0, 2)
+        for q in range(4):
+            nc.sync.dma_start(
+                scale_raw[32 * q : 32 * q + 4, :].bitcast(I32), wb_scales[0, 4 * q : 4 * q + 4, :].bitcast(I32)
+            )
+        nc.sync.dma_start(wb_raw[:].bitcast(I32), wb_words[0].bitcast(I32))
+        load_x(1, 2, 3)
+        load_x(1, 3, 4)
         w_raw = []
         for a in range(PASSES):
             w_raw.append(sb([P, R], I32, "w_raw_%d" % a))
@@ -69,18 +90,8 @@ def tile_list_page_steps_lagged_pl_kernel(
         lag = sb([P, PACK, O], F32, "lag")
         nc.sync.dma_start(lag[:], rs.rearrange("(p t) o -> p t o", t=PACK))
 
-        scale_raw = sb([P, PASSES + 1, R], U8, "scale_raw")
-        nc.gpsimd.memset(scale_raw[:].rearrange("p m c -> p (m c)").bitcast(I32), 0)
-        for q in range(4):
-            nc.gpsimd.dma_start(
-                scale_raw[32 * q : 32 * q + 4, 0:PASSES, :].bitcast(I32),
-                w_scales[:, 4 * q : 4 * q + 4, :].rearrange("a r c -> r a c").bitcast(I32),
-            )
-        for q in range(4):
-            nc.gpsimd.dma_start(
-                scale_raw[32 * q : 32 * q + 4, PASSES, :].bitcast(I32),
-                wb_scales[0, 4 * q : 4 * q + 4, :].bitcast(I32),
-            )
+        scale_full = sb([P, R], U8, "scale_full")
+        nc.vector.memset(scale_full[:].bitcast(I32), 0)
 
         scaled = []
         for a in range(PASSES):
@@ -92,7 +103,7 @@ def tile_list_page_steps_lagged_pl_kernel(
             nc.vector.memset(placed[t][:], 0.0)
 
         u_codes, u_scales = [], []
-        scale_dealt = sb([P, PASSES + 1, PACK, P], U8, "scale_dealt")
+        scale_dealt = sb([P, PACK, P], U8, "scale_dealt")
         wb_dealt = sb([P, PACK, 2 * P], U8, "wb_dealt")
         w_dealt = [sb([P, PACK, P], I32, "w_dealt_%d" % a) for a in range(PASSES)]
 
@@ -105,31 +116,39 @@ def tile_list_page_steps_lagged_pl_kernel(
             u_rows = sb([P, PACK, J], BF16, "u_rows_%d" % a)
             for t in range(PACK):
                 picked = sb([P, J], F32, "picked_%d_%d" % (a, t))
-                nc.scalar.activation(picked[:], x_rows[a, t][:].indirect(token_list[:]), COPY)
-                nc.scalar.activation(scaled[a][:, t, LEAD:], picked[:], COPY, scale=factor[:, a, t : t + 1])
-                if a == PASSES - 1 and t == PACK - 1:
-                    deal_w(0)
+                if a == PASSES - 1 and t >= 2:
+                    nc.vector.tensor_copy(picked[:, :PICK_SPLIT], x_rows[a, t].indirect(token_list[:, : PICK_SPLIT // 16]))
+                    nc.scalar.activation(
+                        picked[:, PICK_SPLIT:], x_rows[a, t].indirect(token_list[:, PICK_SPLIT // 16 :]), COPY
+                    )
+                else:
+                    nc.scalar.activation(picked[:], x_rows[a, t].indirect(token_list[:]), COPY)
+                nc.vector.tensor_scalar(scaled[a][:, t, LEAD:], picked[:], factor[:, a, t : t + 1], None, MULT)
                 nc.vector.scalar_tensor_tensor(
                     u_rows[:, t, :], scaled[a][:, t, LEAD - 1 : LEAD - 1 + J], -0.6, scaled[a][:, t, LEAD:], MULT, ADD
                 )
             if a == PASSES - 1:
-                deal_w(1)
+                deal_w(0)
             u_words = sb([P, J, PACK], BF16, "u_words_%d" % a)
             nc.vector.tensor_copy(u_words[:, :U_SPLIT, :], u_rows[:, :, :U_SPLIT].rearrange("p t j -> p j t"))
             nc.scalar.copy(u_words[:, U_SPLIT:, :], u_rows[:, :, U_SPLIT:].rearrange("p t j -> p j t"))
+            if a == PASSES - 1:
+                deal_w(1)
             u_codes.append(sb([P, J], U32, "u_codes_%d" % a))
             u_scales.append(sb([P, J], U8, "u_scales_%d" % a))
             nc.vector.quantize_mx(
                 out=u_codes[a][:].bitcast(E4M3X4), scales=u_scales[a][:], in_=u_words[:].rearrange("p j t -> p (j t)")
             )
             if a == 0:
+                for q in range(4):
+                    rows = slice(32 * q, 32 * q + 12)
+                    nc.vector.tensor_copy(scale_full[rows].bitcast(I32), scale_raw[rows].bitcast(I32))
                 nc.vector.tensor_copy(
-                    scale_dealt[:].rearrange("p m t q -> p m q t"),
-                    scale_raw[:].rearrange("p m (q t) -> p m q t", t=PACK),
+                    scale_dealt[:].rearrange("p t q -> p q t"), scale_full[:].rearrange("p (q t) -> p q t", t=PACK)
                 )
                 nc.vector.tensor_copy(
-                    wb_dealt[:].rearrange("p t (q b) -> p q t b", b=2),
-                    wb_raw[:].rearrange("p (q t b) -> p q t b", t=PACK, b=2),
+                    wb_dealt[:].bitcast(U16).rearrange("p t q -> p q t"),
+                    wb_raw[:].bitcast(U16).rearrange("p (q t) -> p q t", t=PACK),
                 )
 
         first = [psum.tile([P, J], F32, name="first_%d" % t) for t in range(PACK)]
@@ -138,7 +157,7 @@ def tile_list_page_steps_lagged_pl_kernel(
                 nc.tensor.matmul_mx(
                     out=first[t][:],
                     lhsT=w_dealt[a][:, t, :].bitcast(E4M3X4),
-                    lhsT_scale=scale_dealt[:, a, t, :],
+                    lhsT_scale=scale_dealt[4 * (a + 1) :, t, :],
                     rhs=u_codes[a][:].bitcast(E4M3X4),
                     rhs_scale=u_scales[a][:],
                     start=(a == 0),
@@ -147,38 +166,40 @@ def tile_list_page_steps_lagged_pl_kernel(
 
         ha = [sb([P, J], F32, "ha_%d" % t) for t in range(PACK)]
         page = [sb([P, C], F32, "page_%d" % t) for t in range(PACK)]
-        hid_rows = sb([P, PACK, O], BF16, "hid_rows")
-
-        def relu_on_vector(t):
-            nc.vector.tensor_scalar(ha[t][:], first[t][:], 0.0, None, MAX)
+        hid_rows = [sb([P, PACK, HALF], BF16, "hid_rows_%d" % h) for h in range(2)]
 
         def place_on_scalar(t):
+            nc.scalar.activation(ha[t][:], first[t][:], RELU)
             nc.scalar.activation(placed[t][:].indirect(place_list[:]), ha[t][:], COPY)
 
-        nc.scalar.activation(ha[0][:], first[0][:], RELU)
+        def add_old(t):
+            nc.vector.tensor_tensor(page[t][:], placed[t][:], old[t][:], ADD)
+
+        def read_page(t):
+            nc.vector.tensor_copy(hid_rows[0][:, t, :], page[t][:].indirect(read_list[:, : HALF // 16]))
+            nc.scalar.activation(hid_rows[1][:, t, :], page[t][:].indirect(read_list[:, HALF // 16 :]), COPY)
+
         place_on_scalar(0)
-        relu_on_vector(1)
-        relu_on_vector(2)
+        nc.vector.tensor_scalar(ha[1][:], first[1][:], 0.0, None, MAX)
         nc.vector.tensor_copy(placed[1][:].indirect(place_list[:]), ha[1][:])
-        relu_on_vector(3)
         place_on_scalar(2)
         place_on_scalar(3)
-        for t in range(PACK):
-            nc.vector.tensor_tensor(page[t][:], placed[t][:], old[t][:], ADD)
-        for t in range(PACK - 1):
-            nc.scalar.activation(hid_rows[:, t, :], page[t][:].indirect(read_list[:]), COPY)
-        last = PACK - 1
-        nc.vector.tensor_copy(hid_rows[:, last, :HALF], page[last][:].indirect(read_list[:, : HALF // 16]))
-        nc.scalar.activation(hid_rows[:, last, HALF:], page[last][:].indirect(read_list[:, HALF // 16 :]), COPY)
+        add_old(0)
+        add_old(1)
+        read_page(0)
+        read_page(1)
+        add_old(2)
+        read_page(2)
+        add_old(3)
+        read_page(3)
 
         second = [psum.tile([P, PACK, HALF], F32, name="second_%d" % h) for h in range(2)]
         for h in range(2):
-            cols = slice(h * HALF, (h + 1) * HALF)
             hid_words = sb([P, HALF, PACK], BF16, "hid_words_%d" % h)
             if h == 0:
-                nc.vector.tensor_copy(hid_words[:], hid_rows[:, :, cols].rearrange("p t o -> p o t"))
+                nc.vector.tensor_copy(hid_words[:], hid_rows[h][:].rearrange("p t o -> p o t"))
             else:
-                nc.scalar.copy(hid_words[:], hid_rows[:, :, cols].rearrange("p t o -> p o t"))
+                nc.scalar.copy(hid_words[:], hid_rows[h][:].rearrange("p t o -> p o t"))
             hid_codes = sb([P, HALF], U32, "hid_codes_%d" % h)
             hid_scales = sb([P, HALF], U8, "hid_scales_%d" % h)
             nc.vector.quantize_mx(
@@ -188,7 +209,7 @@ def tile_list_page_steps_lagged_pl_kernel(
                 nc.tensor.matmul_mx(
                     out=second[h][:, t, :],
                     lhsT=wb_dealt[:, t, :].bitcast(E2M1X4),
-                    lhsT_scale=scale_dealt[:, PASSES, t, :],
+                    lhsT_scale=scale_dealt[:, t, :],
                     rhs=hid_codes[:].bitcast(E5M2X4),
                     rhs_scale=hid_scales[:],
                     start=True,
@@ -211,7 +232,8 @@ def tile_list_page_steps_lagged_pl_kernel(
             if h == 0:
                 nc.scalar.copy(y_words[h][:], y[:].rearrange("p t o -> p o t"))
             else:
-                nc.vector.tensor_copy(y_words[h][:], y[:].rearrange("p t o -> p o t"))
+                nc.vector.tensor_copy(y_words[h][:, :Y_SPLIT, :], y[:, :, :Y_SPLIT].rearrange("p t o -> p o t"))
+                nc.scalar.copy(y_words[h][:, Y_SPLIT:, :], y[:, :, Y_SPLIT:].rearrange("p t o -> p o t"))
         for h in range(2):
             cols = slice(h * HALF, (h + 1) * HALF)
             nc.vector.quantize_mx(

@@ -26,9 +26,12 @@ K_PASS = P * PACK
 PASSES = K // K_PASS
 LEAD = 4
 HALF = O // 2
-U_SPLIT = 192
-PICK_SPLIT = 160
+VECTOR_SLOTS = {3: 192}
 Y_SPLIT = 80
+
+
+def weave(copy, words, rows):
+    copy(words.rearrange("p (c i) t -> p c t i", i=4), rows.rearrange("p t (c i) -> p c t i", i=4))
 
 
 def tile_list_page_steps_lagged_pl_kernel(
@@ -53,33 +56,38 @@ def tile_list_page_steps_lagged_pl_kernel(
         wb_raw = sb([P, 2 * N], U8, "wb_raw")
         x_rows = {}
 
-        def load_x(a, t0, t1):
-            chunk = sb([P, t1 - t0, T], F32, "x_rows_%d_%d" % (a, t0))
-            nc.sync.dma_start(
-                chunk[:], xf[a * K_PASS : (a + 1) * K_PASS, :].rearrange("(p t) c -> p t c", t=PACK)[:, t0:t1, :]
-            )
-            for t in range(t0, t1):
-                x_rows[a, t] = chunk[:, t - t0, :]
+        nc.scalar.dma_start(factor[:], fk.rearrange("(a p t) o -> p a (t o)", a=PASSES, t=PACK))
 
-        load_x(0, 0, 1)
-        nc.sync.dma_start(factor[:], fk.rearrange("(a p t) o -> p a (t o)", a=PASSES, t=PACK))
-        load_x(0, 1, 2)
-        load_x(0, 2, 4)
-        for q in range(4):
+        def load_x(n):
+            a, t = divmod(n, PACK)
+            x_rows[a, t] = sb([P, T], F32, "x_rows_%d_%d" % (a, t))
+            nc.sync.dma_start(x_rows[a, t][:], xf[a * K_PASS + t : (a + 1) * K_PASS : PACK, :])
+
+        def load_w_scales(q):
             nc.sync.dma_start(
                 scale_raw[32 * q + 4 : 32 * q + 12, :].bitcast(I32), w_scales[:, 4 * q : 4 * q + 4, :].bitcast(I32)
             )
-        load_x(1, 0, 2)
-        for q in range(4):
+
+        def load_wb_scales(q):
             nc.sync.dma_start(
                 scale_raw[32 * q : 32 * q + 4, :].bitcast(I32), wb_scales[0, 4 * q : 4 * q + 4, :].bitcast(I32)
             )
+
+        load_x(0)
+        for q in range(4):
+            load_w_scales(q)
+        load_x(1)
+        load_x(2)
+        load_wb_scales(0)
+        load_x(3)
+        for q in range(1, 4):
+            load_wb_scales(q)
         nc.sync.dma_start(wb_raw[:].bitcast(I32), wb_words[0].bitcast(I32))
-        load_x(1, 2, 3)
-        load_x(1, 3, 4)
+        for n in range(PACK, PASSES * PACK):
+            load_x(n)
         w_raw = []
         for a in range(PASSES):
-            w_raw.append(sb([P, R], I32, "w_raw_%d" % a))
+            w_raw.append(pool.tile([P, R], I32, name="w_raw_%d" % a, tag="w_raw_%d" % a, align_bytes=64))
             nc.sync.dma_start(w_raw[a][:], w_words[a].rearrange("p c r -> p (c r)").bitcast(I32))
         nc.sync.dma_start(place_list[:], offs2)
         nc.sync.dma_start(read_list[:], offs3)
@@ -95,61 +103,90 @@ def tile_list_page_steps_lagged_pl_kernel(
 
         scaled = []
         for a in range(PASSES):
-            scaled.append(sb([P, PACK, LEAD + J], F32, "scaled_%d" % a))
+            scaled.append(
+                pool.tile([P, PACK, LEAD + J], F32, name="scaled_%d" % a, tag="scaled_%d" % a, align_bytes=64)
+            )
             nc.vector.memset(scaled[a][:, :, LEAD - 1 : LEAD], 0.0)
         placed = []
         for t in range(PACK):
             placed.append(sb([P, C], F32, "placed_%d" % t))
-            nc.vector.memset(placed[t][:], 0.0)
+            nc.gpsimd.memset(placed[t][:], 0.0)
+        spread = {}
+        for t, slots in VECTOR_SLOTS.items():
+            spread[t] = sb([P, slots], F32, "spread_%d" % t)
+            nc.scalar.activation(spread[t][:], factor[:, PASSES - 1, t : t + 1].to_broadcast([P, slots]), COPY)
 
         u_codes, u_scales = [], []
         scale_dealt = sb([P, PACK, P], U8, "scale_dealt")
         wb_dealt = sb([P, PACK, 2 * P], U8, "wb_dealt")
-        w_dealt = [sb([P, PACK, P], I32, "w_dealt_%d" % a) for a in range(PASSES)]
+        w_dealt = {}
 
-        def deal_w(a):
+        def deal_w(a, tag):
+            w_dealt[a] = pool.tile([P, PACK, P], I32, name="w_dealt_%d" % a, tag=tag, align_bytes=64)
             nc.vector.tensor_copy(
-                w_dealt[a][:].rearrange("p t q -> p q t"), w_raw[a][:].rearrange("p (q t) -> p q t", t=PACK)
+                w_dealt[a][:].rearrange("p t (c i) -> p c t i", i=4),
+                w_raw[a][:].rearrange("p (c i t) -> p c t i", i=4, t=PACK),
             )
+
+        for q in range(4):
+            rows = slice(32 * q, 32 * q + 12)
+            nc.vector.tensor_copy(scale_full[rows].bitcast(I32), scale_raw[rows].bitcast(I32))
+        nc.vector.tensor_copy(scale_dealt[:], scale_full[:].rearrange("p (q t) -> p t q", t=PACK))
+        nc.vector.tensor_copy(wb_dealt[:].bitcast(U16), wb_raw[:].bitcast(U16).rearrange("p (q t) -> p t q", t=PACK))
 
         for a in range(PASSES):
             u_rows = sb([P, PACK, J], BF16, "u_rows_%d" % a)
             for t in range(PACK):
-                picked = sb([P, J], F32, "picked_%d_%d" % (a, t))
-                if a == PASSES - 1 and t >= 2:
-                    nc.vector.tensor_copy(picked[:, :PICK_SPLIT], x_rows[a, t].indirect(token_list[:, : PICK_SPLIT // 16]))
-                    nc.scalar.activation(
-                        picked[:, PICK_SPLIT:], x_rows[a, t].indirect(token_list[:, PICK_SPLIT // 16 :]), COPY
+                first_slot = VECTOR_SLOTS.get(t, 0) if a == PASSES - 1 else 0
+                if first_slot:
+                    nc.vector.tensor_tensor(
+                        scaled[a][:, t, LEAD : LEAD + first_slot],
+                        x_rows[a, t][:].indirect(token_list[:, : first_slot // 16]),
+                        spread[t][:],
+                        MULT,
                     )
+                picked = sb([P, J - first_slot], F32, "picked_%d_%d" % (a, t))
+                nc.scalar.activation(picked[:], x_rows[a, t][:].indirect(token_list[:, first_slot // 16 :]), COPY)
+                if t < 2:
+                    nc.vector.tensor_scalar(scaled[a][:, t, LEAD:], picked[:], factor[:, a, t : t + 1], None, MULT)
                 else:
-                    nc.scalar.activation(picked[:], x_rows[a, t].indirect(token_list[:]), COPY)
-                nc.vector.tensor_scalar(scaled[a][:, t, LEAD:], picked[:], factor[:, a, t : t + 1], None, MULT)
-                nc.vector.scalar_tensor_tensor(
-                    u_rows[:, t, :], scaled[a][:, t, LEAD - 1 : LEAD - 1 + J], -0.6, scaled[a][:, t, LEAD:], MULT, ADD
-                )
-            if a == PASSES - 1:
-                deal_w(0)
-            u_words = sb([P, J, PACK], BF16, "u_words_%d" % a)
-            nc.vector.tensor_copy(u_words[:, :U_SPLIT, :], u_rows[:, :, :U_SPLIT].rearrange("p t j -> p j t"))
-            nc.scalar.copy(u_words[:, U_SPLIT:, :], u_rows[:, :, U_SPLIT:].rearrange("p t j -> p j t"))
-            if a == PASSES - 1:
-                deal_w(1)
+                    nc.scalar.activation(
+                        scaled[a][:, t, LEAD + first_slot :], picked[:], COPY, scale=factor[:, a, t : t + 1]
+                    )
+                if t % 2 == 1:
+                    pair = slice(t - 1, t + 1)
+                    nc.vector.scalar_tensor_tensor(
+                        u_rows[:, pair, :],
+                        scaled[a][:, pair, LEAD - 1 : LEAD - 1 + J],
+                        -0.6,
+                        scaled[a][:, pair, LEAD:],
+                        MULT,
+                        ADD,
+                    )
             u_codes.append(sb([P, J], U32, "u_codes_%d" % a))
             u_scales.append(sb([P, J], U8, "u_scales_%d" % a))
-            nc.vector.quantize_mx(
-                out=u_codes[a][:].bitcast(E4M3X4), scales=u_scales[a][:], in_=u_words[:].rearrange("p j t -> p (j t)")
-            )
             if a == 0:
-                for q in range(4):
-                    rows = slice(32 * q, 32 * q + 12)
-                    nc.vector.tensor_copy(scale_full[rows].bitcast(I32), scale_raw[rows].bitcast(I32))
-                nc.vector.tensor_copy(
-                    scale_dealt[:].rearrange("p t q -> p q t"), scale_full[:].rearrange("p (q t) -> p q t", t=PACK)
+                u_words = sb([P, J, PACK], BF16, "u_words")
+                weave(nc.vector.tensor_copy, u_words[:], u_rows[:])
+                nc.vector.quantize_mx(
+                    out=u_codes[a][:].bitcast(E4M3X4),
+                    scales=u_scales[a][:],
+                    in_=u_words[:].rearrange("p j t -> p (j t)"),
                 )
-                nc.vector.tensor_copy(
-                    wb_dealt[:].bitcast(U16).rearrange("p t q -> p q t"),
-                    wb_raw[:].bitcast(U16).rearrange("p (q t) -> p q t", t=PACK),
-                )
+            else:
+                deal_w(0, "w_dealt_0")
+                low = pool.tile([P, J // 2, PACK], BF16, name="u_low", tag="w_raw_0", align_bytes=64)
+                high = sb([P, J // 2, PACK], BF16, "u_high")
+                weave(nc.scalar.copy, high[:], u_rows[:, :, J // 2 :])
+                weave(nc.vector.tensor_copy, low[:], u_rows[:, :, : J // 2])
+                deal_w(1, "scaled_1")
+                for h, half in enumerate((low, high)):
+                    slots = slice(h * J // 2, (h + 1) * J // 2)
+                    nc.vector.quantize_mx(
+                        out=u_codes[a][:, slots].bitcast(E4M3X4),
+                        scales=u_scales[a][:, slots],
+                        in_=half[:].rearrange("p j t -> p (j t)"),
+                    )
 
         first = [psum.tile([P, J], F32, name="first_%d" % t) for t in range(PACK)]
         for a in range(PASSES):
@@ -166,40 +203,38 @@ def tile_list_page_steps_lagged_pl_kernel(
 
         ha = [sb([P, J], F32, "ha_%d" % t) for t in range(PACK)]
         page = [sb([P, C], F32, "page_%d" % t) for t in range(PACK)]
-        hid_rows = [sb([P, PACK, HALF], BF16, "hid_rows_%d" % h) for h in range(2)]
+        hid_rows = sb([P, PACK, O], BF16, "hid_rows")
+
+        def relu_on_vector(t):
+            nc.vector.tensor_scalar(ha[t][:], first[t][:], 0.0, None, MAX)
 
         def place_on_scalar(t):
-            nc.scalar.activation(ha[t][:], first[t][:], RELU)
             nc.scalar.activation(placed[t][:].indirect(place_list[:]), ha[t][:], COPY)
 
-        def add_old(t):
-            nc.vector.tensor_tensor(page[t][:], placed[t][:], old[t][:], ADD)
-
-        def read_page(t):
-            nc.vector.tensor_copy(hid_rows[0][:, t, :], page[t][:].indirect(read_list[:, : HALF // 16]))
-            nc.scalar.activation(hid_rows[1][:, t, :], page[t][:].indirect(read_list[:, HALF // 16 :]), COPY)
-
+        nc.scalar.activation(ha[0][:], first[0][:], RELU)
         place_on_scalar(0)
-        nc.vector.tensor_scalar(ha[1][:], first[1][:], 0.0, None, MAX)
+        relu_on_vector(1)
+        relu_on_vector(2)
         nc.vector.tensor_copy(placed[1][:].indirect(place_list[:]), ha[1][:])
+        relu_on_vector(3)
         place_on_scalar(2)
         place_on_scalar(3)
-        add_old(0)
-        add_old(1)
-        read_page(0)
-        read_page(1)
-        add_old(2)
-        read_page(2)
-        add_old(3)
-        read_page(3)
+        for t in range(PACK):
+            nc.vector.tensor_tensor(page[t][:], placed[t][:], old[t][:], ADD)
+        for t in range(PACK - 1):
+            nc.scalar.activation(hid_rows[:, t, :], page[t][:].indirect(read_list[:]), COPY)
+        last = PACK - 1
+        nc.vector.tensor_copy(hid_rows[:, last, :HALF], page[last][:].indirect(read_list[:, : HALF // 16]))
+        nc.scalar.activation(hid_rows[:, last, HALF:], page[last][:].indirect(read_list[:, HALF // 16 :]), COPY)
 
         second = [psum.tile([P, PACK, HALF], F32, name="second_%d" % h) for h in range(2)]
         for h in range(2):
+            cols = slice(h * HALF, (h + 1) * HALF)
             hid_words = sb([P, HALF, PACK], BF16, "hid_words_%d" % h)
             if h == 0:
-                nc.vector.tensor_copy(hid_words[:], hid_rows[h][:].rearrange("p t o -> p o t"))
+                weave(nc.vector.tensor_copy, hid_words[:], hid_rows[:, :, cols])
             else:
-                nc.scalar.copy(hid_words[:], hid_rows[h][:].rearrange("p t o -> p o t"))
+                weave(nc.scalar.copy, hid_words[:], hid_rows[:, :, cols])
             hid_codes = sb([P, HALF], U32, "hid_codes_%d" % h)
             hid_scales = sb([P, HALF], U8, "hid_scales_%d" % h)
             nc.vector.quantize_mx(
@@ -230,10 +265,10 @@ def tile_list_page_steps_lagged_pl_kernel(
             nc.sync.dma_start(out_rows[:, :, cols], y[:])
             y_words.append(sb([P, HALF, PACK], BF16, "y_words_%d" % h))
             if h == 0:
-                nc.scalar.copy(y_words[h][:], y[:].rearrange("p t o -> p o t"))
+                weave(nc.scalar.copy, y_words[h][:], y[:])
             else:
-                nc.vector.tensor_copy(y_words[h][:, :Y_SPLIT, :], y[:, :, :Y_SPLIT].rearrange("p t o -> p o t"))
-                nc.scalar.copy(y_words[h][:, Y_SPLIT:, :], y[:, :, Y_SPLIT:].rearrange("p t o -> p o t"))
+                weave(nc.vector.tensor_copy, y_words[h][:, :Y_SPLIT, :], y[:, :, :Y_SPLIT])
+                weave(nc.scalar.copy, y_words[h][:, Y_SPLIT:, :], y[:, :, Y_SPLIT:])
         for h in range(2):
             cols = slice(h * HALF, (h + 1) * HALF)
             nc.vector.quantize_mx(

from contextlib import ExitStack

import concourse.mybir as mybir

K, T, J, R, C, O, N = 1024, 1024, 256, 512, 1024, 256, 512
FLOPS = 2 * K * R * J + 2 * R * N * O

F32 = mybir.dt.float32
BF16 = mybir.dt.bfloat16
I32 = mybir.dt.int32
U32 = mybir.dt.uint32
U16 = mybir.dt.uint16
U8 = mybir.dt.uint8
E4M3X4 = mybir.dt.float8_e4m3fn_x4
E5M2X4 = mybir.dt.float8_e5m2_x4
E2M1X4 = mybir.dt.float4_e2m1fn_x4
MULT = mybir.AluOpType.mult
ADD = mybir.AluOpType.add
MAX = mybir.AluOpType.max
COPY = mybir.ActivationFunctionType.Copy
RELU = mybir.ActivationFunctionType.Relu

P = 128
PACK = 4
K_PASS = P * PACK
PASSES = K // K_PASS
LEAD = 4
HALF = O // 2
VECTOR_SLOTS = {3: 192}
Y_SPLIT = 80


def weave(copy, words, rows):
    copy(words.rearrange("p (c i) t -> p c t i", i=4), rows.rearrange("p t (c i) -> p c t i", i=4))


def tile_list_page_steps_lagged_pl_kernel(
    tc, xf, fk, w_words, w_scales, oldh, wb_words, wb_scales, rs, offs, offs2, offs3, out_0, out_1, out_2
):
    nc = tc.nc
    with ExitStack() as ctx:
        lists = ctx.enter_context(tc.tile_pool(name="lists", bufs=1))
        pool = ctx.enter_context(tc.tile_pool(name="pool", bufs=1))
        psum = ctx.enter_context(tc.psum_pool(name="psum", bufs=1))

        def sb(shape, dtype, name):
            return pool.tile(shape, dtype, name=name, align_bytes=64)

        token_list = lists.tile([P, J // 16], U16, name="token_list")
        place_list = lists.tile([P, J // 16], U16, name="place_list")
        read_list = lists.tile([P, O // 16], U16, name="read_list")

        nc.sync.dma_start(token_list[:], offs)
        factor = sb([P, PASSES, PACK], F32, "factor")
        scale_raw = sb([P, R], U8, "scale_raw")
        wb_raw = sb([P, 2 * N], U8, "wb_raw")
        x_rows = {}

        nc.scalar.dma_start(factor[:], fk.rearrange("(a p t) o -> p a (t o)", a=PASSES, t=PACK))

        def load_x(n):
            a, t = divmod(n, PACK)
            x_rows[a, t] = sb([P, T], F32, "x_rows_%d_%d" % (a, t))
            nc.sync.dma_start(x_rows[a, t][:], xf[a * K_PASS + t : (a + 1) * K_PASS : PACK, :])

        def load_w_scales(q):
            nc.sync.dma_start(
                scale_raw[32 * q + 4 : 32 * q + 12, :].bitcast(I32), w_scales[:, 4 * q : 4 * q + 4, :].bitcast(I32)
            )

        def load_wb_scales(q):
            nc.sync.dma_start(
                scale_raw[32 * q : 32 * q + 4, :].bitcast(I32), wb_scales[0, 4 * q : 4 * q + 4, :].bitcast(I32)
            )

        load_x(0)
        for q in range(4):
            load_w_scales(q)
        load_x(1)
        load_x(2)
        load_wb_scales(0)
        load_x(3)
        for q in range(1, 4):
            load_wb_scales(q)
        nc.sync.dma_start(wb_raw[:].bitcast(I32), wb_words[0].bitcast(I32))
        for n in range(PACK, PASSES * PACK):
            load_x(n)
        w_raw = []
        for a in range(PASSES):
            w_raw.append(pool.tile([P, R], I32, name="w_raw_%d" % a, tag="w_raw_%d" % a, align_bytes=64))
            nc.sync.dma_start(w_raw[a][:], w_words[a].rearrange("p c r -> p (c r)").bitcast(I32))
        nc.sync.dma_start(place_list[:], offs2)
        nc.sync.dma_start(read_list[:], offs3)
        old = []
        for t in range(PACK):
            old.append(sb([P, C], F32, "old_%d" % t))
            nc.sync.dma_start(old[t][:], oldh[t:R:PACK, :])
        lag = sb([P, PACK, O], F32, "lag")
        nc.sync.dma_start(lag[:], rs.rearrange("(p t) o -> p t o", t=PACK))

        scale_full = sb([P, R], U8, "scale_full")
        nc.vector.memset(scale_full[:].bitcast(I32), 0)

        scaled = []
        for a in range(PASSES):
            scaled.append(
                pool.tile([P, PACK, LEAD + J], F32, name="scaled_%d" % a, tag="scaled_%d" % a, align_bytes=64)
            )
            nc.vector.memset(scaled[a][:, :, LEAD - 1 : LEAD], 0.0)
        placed = []
        for t in range(PACK):
            placed.append(sb([P, C], F32, "placed_%d" % t))
            nc.gpsimd.memset(placed[t][:], 0.0)
        spread = {}
        for t, slots in VECTOR_SLOTS.items():
            spread[t] = sb([P, slots], F32, "spread_%d" % t)
            nc.scalar.activation(spread[t][:], factor[:, PASSES - 1, t : t + 1].to_broadcast([P, slots]), COPY)

        u_codes, u_scales = [], []
        scale_dealt = sb([P, PACK, P], U8, "scale_dealt")
        wb_dealt = sb([P, PACK, 2 * P], U8, "wb_dealt")
        w_dealt = {}

        def deal_w(a, tag):
            w_dealt[a] = pool.tile([P, PACK, P], I32, name="w_dealt_%d" % a, tag=tag, align_bytes=64)
            nc.vector.tensor_copy(
                w_dealt[a][:].rearrange("p t (c i) -> p c t i", i=4),
                w_raw[a][:].rearrange("p (c i t) -> p c t i", i=4, t=PACK),
            )

        for q in range(4):
            rows = slice(32 * q, 32 * q + 12)
            nc.vector.tensor_copy(scale_full[rows].bitcast(I32), scale_raw[rows].bitcast(I32))
        nc.vector.tensor_copy(scale_dealt[:], scale_full[:].rearrange("p (q t) -> p t q", t=PACK))
        nc.vector.tensor_copy(wb_dealt[:].bitcast(U16), wb_raw[:].bitcast(U16).rearrange("p (q t) -> p t q", t=PACK))

        for a in range(PASSES):
            u_rows = sb([P, PACK, J], BF16, "u_rows_%d" % a)
            for t in range(PACK):
                first_slot = VECTOR_SLOTS.get(t, 0) if a == PASSES - 1 else 0
                if first_slot:
                    nc.vector.tensor_tensor(
                        scaled[a][:, t, LEAD : LEAD + first_slot],
                        x_rows[a, t][:].indirect(token_list[:, : first_slot // 16]),
                        spread[t][:],
                        MULT,
                    )
                picked = sb([P, J - first_slot], F32, "picked_%d_%d" % (a, t))
                nc.scalar.activation(picked[:], x_rows[a, t][:].indirect(token_list[:, first_slot // 16 :]), COPY)
                if t < 2:
                    nc.vector.tensor_scalar(scaled[a][:, t, LEAD:], picked[:], factor[:, a, t : t + 1], None, MULT)
                else:
                    nc.scalar.activation(
                        scaled[a][:, t, LEAD + first_slot :], picked[:], COPY, scale=factor[:, a, t : t + 1]
                    )
                if t % 2 == 1:
                    pair = slice(t - 1, t + 1)
                    nc.vector.scalar_tensor_tensor(
                        u_rows[:, pair, :],
                        scaled[a][:, pair, LEAD - 1 : LEAD - 1 + J],
                        -0.6,
                        scaled[a][:, pair, LEAD:],
                        MULT,
                        ADD,
                    )
            u_codes.append(sb([P, J], U32, "u_codes_%d" % a))
            u_scales.append(sb([P, J], U8, "u_scales_%d" % a))
            if a == 0:
                u_words = sb([P, J, PACK], BF16, "u_words")
                weave(nc.vector.tensor_copy, u_words[:], u_rows[:])
                nc.vector.quantize_mx(
                    out=u_codes[a][:].bitcast(E4M3X4),
                    scales=u_scales[a][:],
                    in_=u_words[:].rearrange("p j t -> p (j t)"),
                )
            else:
                deal_w(0, "w_dealt_0")
                low = pool.tile([P, J // 2, PACK], BF16, name="u_low", tag="w_raw_0", align_bytes=64)
                high = sb([P, J // 2, PACK], BF16, "u_high")
                weave(nc.scalar.copy, high[:], u_rows[:, :, J // 2 :])
                weave(nc.vector.tensor_copy, low[:], u_rows[:, :, : J // 2])
                deal_w(1, "scaled_1")
                for h, half in enumerate((low, high)):
                    slots = slice(h * J // 2, (h + 1) * J // 2)
                    nc.vector.quantize_mx(
                        out=u_codes[a][:, slots].bitcast(E4M3X4),
                        scales=u_scales[a][:, slots],
                        in_=half[:].rearrange("p j t -> p (j t)"),
                    )

        first = [psum.tile([P, J], F32, name="first_%d" % t) for t in range(PACK)]
        for a in range(PASSES):
            for t in range(PACK):
                nc.tensor.matmul_mx(
                    out=first[t][:],
                    lhsT=w_dealt[a][:, t, :].bitcast(E4M3X4),
                    lhsT_scale=scale_dealt[4 * (a + 1) :, t, :],
                    rhs=u_codes[a][:].bitcast(E4M3X4),
                    rhs_scale=u_scales[a][:],
                    start=(a == 0),
                    stop=(a == PASSES - 1),
                )

        ha = [sb([P, J], F32, "ha_%d" % t) for t in range(PACK)]
        page = [sb([P, C], F32, "page_%d" % t) for t in range(PACK)]
        hid_rows = sb([P, PACK, O], BF16, "hid_rows")

        def relu_on_vector(t):
            nc.vector.tensor_scalar(ha[t][:], first[t][:], 0.0, None, MAX)

        def place_on_scalar(t):
            nc.scalar.activation(placed[t][:].indirect(place_list[:]), ha[t][:], COPY)

        nc.scalar.activation(ha[0][:], first[0][:], RELU)
        place_on_scalar(0)
        relu_on_vector(1)
        relu_on_vector(2)
        nc.vector.tensor_copy(placed[1][:].indirect(place_list[:]), ha[1][:])
        relu_on_vector(3)
        place_on_scalar(2)
        place_on_scalar(3)
        for t in range(PACK):
            nc.vector.tensor_tensor(page[t][:], placed[t][:], old[t][:], ADD)
        for t in range(PACK - 1):
            nc.scalar.activation(hid_rows[:, t, :], page[t][:].indirect(read_list[:]), COPY)
        last = PACK - 1
        nc.vector.tensor_copy(hid_rows[:, last, :HALF], page[last][:].indirect(read_list[:, : HALF // 16]))
        nc.scalar.activation(hid_rows[:, last, HALF:], page[last][:].indirect(read_list[:, HALF // 16 :]), COPY)

        second = [psum.tile([P, PACK, HALF], F32, name="second_%d" % h) for h in range(2)]
        for h in range(2):
            cols = slice(h * HALF, (h + 1) * HALF)
            hid_words = sb([P, HALF, PACK], BF16, "hid_words_%d" % h)
            if h == 0:
                weave(nc.vector.tensor_copy, hid_words[:], hid_rows[:, :, cols])
            else:
                weave(nc.scalar.copy, hid_words[:], hid_rows[:, :, cols])
            hid_codes = sb([P, HALF], U32, "hid_codes_%d" % h)
            hid_scales = sb([P, HALF], U8, "hid_scales_%d" % h)
            nc.vector.quantize_mx(
                out=hid_codes[:].bitcast(E5M2X4), scales=hid_scales[:], in_=hid_words[:].rearrange("p o t -> p (o t)")
            )
            for t in range(PACK):
                nc.tensor.matmul_mx(
                    out=second[h][:, t, :],
                    lhsT=wb_dealt[:, t, :].bitcast(E2M1X4),
                    lhsT_scale=scale_dealt[:, t, :],
                    rhs=hid_codes[:].bitcast(E5M2X4),
                    rhs_scale=hid_scales[:],
                    start=True,
                    stop=True,
                )

        y_codes = sb([P, O], U32, "y_codes")
        y_scales = sb([P, O], U8, "y_scales")
        out_rows = out_0.rearrange("(p t) o -> p t o", t=PACK)
        y_words = []
        for h in range(2):
            cols = slice(h * HALF, (h + 1) * HALF)
            width = min(HALF, O - 1 - h * HALF)
            ahead = lag[:, :, h * HALF + 1 : h * HALF + 1 + width]
            nc.vector.scalar_tensor_tensor(ahead, second[h][:, :, :width], -1.4, ahead, MULT, ADD)
            y = sb([P, PACK, HALF], F32, "y_%d" % h)
            nc.vector.scalar_tensor_tensor(y[:], lag[:, :, cols], 0.5, second[h][:], MULT, ADD)
            nc.sync.dma_start(out_rows[:, :, cols], y[:])
            y_words.append(sb([P, HALF, PACK], BF16, "y_words_%d" % h))
            if h == 0:
                weave(nc.scalar.copy, y_words[h][:], y[:])
            else:
                weave(nc.vector.tensor_copy, y_words[h][:, :Y_SPLIT, :], y[:, :, :Y_SPLIT])
                weave(nc.scalar.copy, y_words[h][:, Y_SPLIT:, :], y[:, :, Y_SPLIT:])
        for h in range(2):
            cols = slice(h * HALF, (h + 1) * HALF)
            nc.vector.quantize_mx(
                out=y_codes[:, cols].bitcast(E4M3X4),
                scales=y_scales[:, cols],
                in_=y_words[h][:].rearrange("p o t -> p (o t)"),
            )
        nc.sync.dma_start(out_1[0].rearrange("p c r -> p (c r)").bitcast(I32), y_codes[:].bitcast(I32))
        for q in range(4):
            engine = nc.scalar if q % 2 == 0 else nc.sync
            engine.dma_start(
                out_2[0, 4 * q : 4 * q + 4, :].bitcast(I32), y_scales[32 * q : 32 * q + 4, :].bitcast(I32)
            )
